import numpy as np, ml_dtypes
CORES = [26,28,98,100,106,108,122,124]
N = 8
import mx_ref
NC, KT = 512, 1
BF = ml_dtypes.bfloat16
def setup_inputs(rng):
    def f(*shape):
        return mx_ref.flush((rng.standard_normal(shape, dtype=np.float32) * np.exp2(rng.integers(-2, 3, shape[:-1] + (1,)))).astype(BF))
    return {"w": f(N, 128, KT * 512), "x": f(N, 128, KT * 4 * NC)}
def setup_inputs_blocks(rng):
    d = setup_inputs(rng)
    for k in ("w", "x"): d[k] = mx_ref.spread(d[k], rng, 4)
    return d
def setup_inputs_wide(rng):
    d = setup_inputs(rng)
    for k in ("w", "x"): d[k] = mx_ref.flush((d[k].astype(np.float32) * np.exp2(rng.integers(-8, 9, (N, 1, 1))).astype(np.float32)).astype(BF))
    return d
def setup_inputs_zeros(rng):
    d = setup_inputs(rng); v = d["x"].reshape(N, 128, -1, 4).copy()
    v[np.broadcast_to((rng.random((N, 1, v.shape[2], 1)) < 0.33), v.shape)] = 0
    d["x"] = v.reshape(d["x"].shape)
    return d
def reference(w, x):
    QW = [[mx_ref.quantize(w[r][:, 512 * t:512 * t + 512]) for t in range(KT)] for r in range(N)]
    QX = [[mx_ref.quantize(x[j][:, 4 * NC * t:4 * NC * t + 4 * NC]) for t in range(KT)] for j in range(N)]
    y = np.zeros((N, 128, N * NC), np.float32)
    for r in range(N):
        for j in range(N):
            for t in range(KT):
                p = mx_ref.matmul(QW[r][t], QX[j][t])
                y[r][:, NC * j:NC * j + NC] = p if t == 0 else y[r][:, NC * j:NC * j + NC] + p
    return {"y": y}

@@ -1,0 +1,256 @@
+from concourse.bass import DstId, RemoteDMATransfer
+from concourse.mybir import dt, ActivationFunctionType
+
+N = 8
+NC = 512
+NCORES = 128
+NCHIPS = 16
+
+CFG = {
+    "recv": "helper",
+    "idle_relay": True,
+    "gate_all": True,
+    "fine": True,
+    "near_engines": 16,
+    "far_engines": 8,
+    "pair_store": False,
+}
+PIECE = {"c0": ("c", 0, 128), "c1": ("c", 128, 512), "c": ("c", 0, 512), "p": ("p", 0, 512)}
+FINE = ("c0", "p", "c1")
+COARSE = ("p", "c")
+CUTS = ((0, 128), (128, 512))
+
+SCRATCH = {
+    "xb": ("sbuf", [128, 4 * NC], "bfloat16"),
+    "wb": ("sbuf", [128, 512], "bfloat16"),
+    "wq": ("sbuf", [128, 128], "float8_e4m3fn_x4"),
+    "ws": ("sbuf", [128, 128], "uint8"),
+    "xq": ("sbuf", [128, N * NC], "float8_e4m3fn_x4"),
+    "xs": ("sbuf", [128, N * NC], "uint8"),
+    "yb": ("sbuf", [128, N * NC], "float32"),
+    "ps": ("psum", [128, N * NC], "float32"),
+}
+SEMAPHORES = (["lw", "qw", "sent", "st_s", "st_a"]
+              + ["lx%d" % i for i in range(len(CUTS))] + ["qx%d" % i for i in range(len(CUTS))]
+              + ["a%d_%s" % (j, n) for j in range(N) for n in PIECE]
+              + ["mm%d" % j for j in range(N)] + ["ev%d" % j for j in range(N)])
+
+
+def _bits(mask):
+    return bin(mask).count("1")
+
+
+def _trim(mask, k):
+    out = 0
+    for b in range(mask.bit_length()):
+        if mask >> b & 1 and _bits(out) < k:
+            out |= 1 << b
+    return out
+
+
+def _groups(topo, p, kids):
+    far = [c for c in kids if topo.chip(c) != topo.chip(p)]
+    near = [c for c in kids if topo.chip(c) == topo.chip(p)]
+    out, far_mask = [], 0
+    if far:
+        far_mask = topo.mask(p, far[0])
+        out.append((_trim(far_mask, CFG["far_engines"]), far))
+    if near:
+        out.append((_trim(topo.mask(p, near[0]) & ~far_mask, CFG["near_engines"]), near))
+    return out
+
+
+def _plan(ranks, topo):
+    chip, die = topo.chip, topo.die
+    homes = []
+    for c in ranks:
+        if chip(c) not in homes:
+            homes.append(chip(c))
+    at = {ch: [c for c in ranks if chip(c) == ch] for ch in homes}
+    load = {}
+
+    def free(ch, d, towards=None):
+        ok = [c for c in range(NCORES) if chip(c) == ch and die(c) == d and c not in ranks
+              and (towards is None or topo.may_write(c, towards))]
+        c = min(ok, key=lambda c: load.get(c, 0))
+        load[c] = load.get(c, 0) + 1
+        return c
+
+    gate = {}
+    for s in ranks:
+        other = [t for t in ranks if chip(t) != chip(s) and not topo.same_plane(chip(s), chip(t))]
+        barred = [t for t in other if not topo.may_write(s, t)]
+        gate[s] = free(chip(s), die(s), other[0]) if barred or CFG["gate_all"] else s
+
+    kids, fmt, when = [], [], []
+    for j, s in enumerate(ranks):
+        k = {}
+
+        def link(a, b):
+            if a != b and b not in k.setdefault(a, []):
+                k[a].append(b)
+
+        def spread(a, ch):
+            if CFG["recv"] == "both":
+                for t in at[ch]:
+                    link(a, t)
+                return
+            if CFG["recv"] == "rank":
+                h = [t for t in at[ch] if die(t) == die(a)][0]
+            else:
+                h = free(ch, die(a))
+            link(a, h)
+            for t in at[ch]:
+                link(h, t)
+
+        cs = chip(s)
+        for t in at[cs]:
+            link(s, t)
+        i = homes.index(cs)
+        for ch in homes[i + 1:] + homes[:i]:
+            if topo.same_plane(cs, ch):
+                spread(s, ch)
+            elif topo.mates(cs, ch):
+                link(s, gate[s])
+                for t in at[ch]:
+                    link(gate[s], t)
+            else:
+                m = [c for c in range(NCHIPS) if topo.mates(c, ch)][0]
+                if CFG["idle_relay"] and m not in homes:
+                    h = free(m, die(s), at[ch][0])
+                    link(s, h)
+                    for t in at[ch]:
+                        link(h, t)
+                else:
+                    link(s, gate[s])
+                    spread(gate[s], ch)
+
+        def depth(c):
+            return 1 + max([depth(x) for x in k[c]]) if c in k else 0
+
+        for p in k:
+            k[p] = sorted(k[p], key=lambda c: -depth(c))
+        w, f = {s: 0.0}, {}
+
+        def walk(p):
+            for mask, grp in _groups(topo, p, k[p]):
+                for n, c in enumerate(grp):
+                    w[c] = w[p] + 1.0 + (n + 1) * (1.0 if chip(c) != chip(p) else 0.5)
+                    f[c] = f[p] if p != s else (FINE if chip(c) == cs and CFG["fine"] else COARSE)
+                    if c in k:
+                        walk(c)
+        walk(s)
+        kids.append(k)
+        fmt.append(f)
+        when.append(w)
+    return kids, fmt, when
+
+
+def _view(T, j, name):
+    kind, lo, hi = PIECE[name]
+    if kind == "c":
+        return T.xq[:, j * NC + lo:j * NC + hi].bitcast(dt.uint8)
+    return T.xs[:, j * NC + lo:j * NC + hi]
+
+
+def _send(g, T, topo, j, name, groups):
+    v = _view(T, j, name)
+    trs = []
+    for mask, grp in groups:
+        ids = [DstId(rid=topo.addr(c)[0], pnc=topo.addr(c)[1]) for c in grp]
+        trs.append(RemoteDMATransfer(dst_ids=ids, dma_engine_mask=mask, remote_sem=T.sem["a%d_%s" % (j, name)],
+                                     srcs=[v], dsts=[v for c in grp]))
+    g.remote_dma_fused(trs, local_sem=T.sem.sent)
+    return sum(_bits(mask) for mask, grp in groups)
+
+
+def _lands(topo, kids, j, c):
+    for p in kids[j]:
+        for mask, grp in _groups(topo, p, kids[j][p]):
+            if c in grp:
+                return _bits(mask)
+    return 0
+
+
+def rank_program(g, core, T, topo):
+    ranks = list(T.cores)
+    kids, fmt, when = _plan(ranks, topo)
+    S = T.sem
+    r = T.rank_of(core)
+
+    if r is not None:
+        for i, (lo, hi) in enumerate(CUTS):
+            g.sync.dma_start(T.xb[:, 4 * lo:4 * hi], T.x[:, 4 * lo:4 * hi]).then_inc(S["lx%d" % i], 16)
+        g.sync.dma_start(T.wb[:], T.w[:]).then_inc(S.lw, 16)
+        for i, (lo, hi) in enumerate(CUTS):
+            g.vector.wait_ge(S["lx%d" % i], 16)
+            g.vector.quantize_mx(T.xq[:, r * NC + lo:r * NC + hi], T.xs[:, r * NC + lo:r * NC + hi],
+                                 T.xb[:, 4 * lo:4 * hi]).then_inc(S["qx%d" % i], 1)
+        g.vector.wait_ge(S.lw, 16)
+        g.vector.quantize_mx(T.wq[:], T.ws[:], T.wb[:]).then_inc(S.qw, 1)
+
+    sent = 0
+    flows = sorted([j for j in range(N) if core in kids[j]], key=lambda j: when[j][core])
+    for j in flows:
+        groups = _groups(topo, core, kids[j][core])
+        if j == r:
+            far = [(m, grp) for m, grp in groups if topo.chip(grp[0]) != topo.chip(core)]
+            near = [(m, grp) for m, grp in groups if topo.chip(grp[0]) == topo.chip(core)]
+            g.wait_ge(S.qx0, 1)
+            if CFG["fine"]:
+                sent += _send(g, T, topo, j, "c0", near)
+            g.wait_ge(S.qx1, 1)
+            sent += _send(g, T, topo, j, "p", groups)
+            if CFG["fine"]:
+                sent += _send(g, T, topo, j, "c1", near)
+            first = [] if CFG["fine"] else near
+            for m, grp in far:
+                for c in grp:
+                    sent += _send(g, T, topo, j, "c", [(m, [c])] + first)
+                    first = []
+            if first:
+                sent += _send(g, T, topo, j, "c", first)
+        else:
+            for name in fmt[j][core]:
+                g.wait_ge(S["a%d_%s" % (j, name)], _lands(topo, kids, j, core))
+                sent += _send(g, T, topo, j, name, groups)
+    if sent:
+        g.wait_ge(S.sent, sent)
+    if r is None:
+        return
+
+    order = sorted(range(N), key=lambda j: when[j][core])
+    g.tensor.wait_ge(S.qw, 1)
+    for j in order:
+        if j == r:
+            for q in range(len(CUTS)):
+                g.tensor.wait_ge(S["qx%d" % q], 1)
+        else:
+            for name in fmt[j][core]:
+                g.tensor.wait_ge(S["a%d_%s" % (j, name)], _lands(topo, kids, j, core))
+        blk = slice(j * NC, (j + 1) * NC)
+        g.tensor.matmul_mx(T.ps[:, blk], T.wq[:], T.ws[:], T.xq[:, blk], T.xs[:, blk], True, True).then_inc(S["mm%d" % j], 1)
+    ns = na = 0
+    for n, j in enumerate(order):
+        blk = slice(j * NC, (j + 1) * NC)
+        twin = order[n ^ 1]
+        paired = CFG["pair_store"] and twin == j ^ 1
+        if n % 2 == 0:
+            g.vector.wait_ge(S["mm%d" % j], 1)
+            g.vector.tensor_copy(T.yb[:, blk], T.ps[:, blk]).then_inc(S["ev%d" % j], 1)
+            g.sync.wait_ge(S["ev%d" % j], 1)
+            if paired:
+                g.sync.wait_ge(S["ev%d" % twin], 1)
+                blk = slice(min(j, twin) * NC, (max(j, twin) + 1) * NC)
+            g.sync.dma_start(T.y[:, blk], T.yb[:, blk]).then_inc(S.st_s, 16)
+            ns += 16
+        else:
+            g.scalar.wait_ge(S["mm%d" % j], 1)
+            g.scalar.activation(T.yb[:, blk], T.ps[:, blk], ActivationFunctionType.Copy).then_inc(S["ev%d" % j], 1)
+            if not paired:
+                g.scalar.wait_ge(S["ev%d" % j], 1)
+                g.scalar.dma_start(T.y[:, blk], T.yb[:, blk]).then_inc(S.st_a, 16)
+                na += 16
+    g.sync.wait_ge(S.st_s, ns)
+    if na:
+        g.scalar.wait_ge(S.st_a, na)

@@ -3,22 +3,17 @@ from concourse.mybir import dt, ActivationFunctionType
 
 N = 8
 NC = 512
+HEAD = 128
+MID = 320
 NCORES = 128
 NCHIPS = 16
+BANKS = 8
+NMM = 2 * N - 1
 
-CFG = {
-    "recv": "helper",
-    "idle_relay": True,
-    "gate_all": True,
-    "fine": True,
-    "near_engines": 16,
-    "far_engines": 8,
-    "pair_store": False,
-}
-PIECE = {"c0": ("c", 0, 128), "c1": ("c", 128, 512), "c": ("c", 0, 512), "p": ("p", 0, 512)}
-FINE = ("c0", "p", "c1")
-COARSE = ("p", "c")
-CUTS = ((0, 128), (128, 512))
+PIECE = {"c0": ("c", 0, HEAD), "p": ("p", 0, NC), "c1": ("c", HEAD, MID), "c2": ("c", MID, NC)}
+ORDER = ("c0", "p", "c1", "c2")
+LAG = (0.0, 1.5, 2.0, 2.75)
+CUTS = ((0, HEAD), (HEAD, NC))
 
 SCRATCH = {
     "xb": ("sbuf", [128, 4 * NC], "bfloat16"),
@@ -28,24 +23,16 @@ SCRATCH = {
     "xq": ("sbuf", [128, N * NC], "float8_e4m3fn_x4"),
     "xs": ("sbuf", [128, N * NC], "uint8"),
     "yb": ("sbuf", [128, N * NC], "float32"),
-    "ps": ("psum", [128, N * NC], "float32"),
+    "ps": ("psum", [128, BANKS * NC], "float32"),
 }
 SEMAPHORES = (["lw", "qw", "sent", "st_s", "st_a"]
               + ["lx%d" % i for i in range(len(CUTS))] + ["qx%d" % i for i in range(len(CUTS))]
               + ["a%d_%s" % (j, n) for j in range(N) for n in PIECE]
-              + ["mm%d" % j for j in range(N)] + ["ev%d" % j for j in range(N)])
+              + ["mm%d" % i for i in range(NMM)] + ["ev%d" % i for i in range(NMM)])
 
 
 def _bits(mask):
     return bin(mask).count("1")
-
-
-def _trim(mask, k):
-    out = 0
-    for b in range(mask.bit_length()):
-        if mask >> b & 1 and _bits(out) < k:
-            out |= 1 << b
-    return out
 
 
 def _groups(topo, p, kids):
@@ -54,9 +41,9 @@ def _groups(topo, p, kids):
     out, far_mask = [], 0
     if far:
         far_mask = topo.mask(p, far[0])
-        out.append((_trim(far_mask, CFG["far_engines"]), far))
+        out.append((far_mask, far))
     if near:
-        out.append((_trim(topo.mask(p, near[0]) & ~far_mask, CFG["near_engines"]), near))
+        out.append((topo.mask(p, near[0]) & ~far_mask, near))
     return out
 
 
@@ -69,9 +56,9 @@ def _plan(ranks, topo):
     at = {ch: [c for c in ranks if chip(c) == ch] for ch in homes}
     load = {}
 
-    def free(ch, d, towards=None):
+    def free(ch, d, towards):
         ok = [c for c in range(NCORES) if chip(c) == ch and die(c) == d and c not in ranks
-              and (towards is None or topo.may_write(c, towards))]
+              and topo.may_write(c, towards)]
         c = min(ok, key=lambda c: load.get(c, 0))
         load[c] = load.get(c, 0) + 1
         return c
@@ -79,10 +66,9 @@ def _plan(ranks, topo):
     gate = {}
     for s in ranks:
         other = [t for t in ranks if chip(t) != chip(s) and not topo.same_plane(chip(s), chip(t))]
-        barred = [t for t in other if not topo.may_write(s, t)]
-        gate[s] = free(chip(s), die(s), other[0]) if barred or CFG["gate_all"] else s
+        gate[s] = free(chip(s), die(s), other[0])
 
-    kids, fmt, when = [], [], []
+    kids, when = [], []
     for j, s in enumerate(ranks):
         k = {}
 
@@ -91,14 +77,7 @@ def _plan(ranks, topo):
                 k[a].append(b)
 
         def spread(a, ch):
-            if CFG["recv"] == "both":
-                for t in at[ch]:
-                    link(a, t)
-                return
-            if CFG["recv"] == "rank":
-                h = [t for t in at[ch] if die(t) == die(a)][0]
-            else:
-                h = free(ch, die(a))
+            h = [t for t in at[ch] if die(t) == die(a)][0]
             link(a, h)
             for t in at[ch]:
                 link(h, t)
@@ -107,43 +86,38 @@ def _plan(ranks, topo):
         for t in at[cs]:
             link(s, t)
         i = homes.index(cs)
-        for ch in homes[i + 1:] + homes[:i]:
+        ring = homes[i + 1:] + homes[:i]
+        if die(s) != die(ranks[0]):
+            ring = ring[::-1]
+        for ch in ring:
             if topo.same_plane(cs, ch):
                 spread(s, ch)
-            elif topo.mates(cs, ch):
-                link(s, gate[s])
-                for t in at[ch]:
-                    link(gate[s], t)
+                continue
+            m = [c for c in range(NCHIPS) if topo.mates(c, ch)][0]
+            if m != cs and m not in homes:
+                h = free(m, die(s), at[ch][0])
             else:
-                m = [c for c in range(NCHIPS) if topo.mates(c, ch)][0]
-                if CFG["idle_relay"] and m not in homes:
-                    h = free(m, die(s), at[ch][0])
-                    link(s, h)
-                    for t in at[ch]:
-                        link(h, t)
-                else:
-                    link(s, gate[s])
-                    spread(gate[s], ch)
+                h = gate[s]
+            link(s, h)
+            spread(h, ch)
 
         def depth(c):
             return 1 + max([depth(x) for x in k[c]]) if c in k else 0
 
         for p in k:
             k[p] = sorted(k[p], key=lambda c: -depth(c))
-        w, f = {s: 0.0}, {}
+        w = {s: 0.0}
 
         def walk(p):
             for mask, grp in _groups(topo, p, k[p]):
                 for n, c in enumerate(grp):
                     w[c] = w[p] + 1.0 + (n + 1) * (1.0 if chip(c) != chip(p) else 0.5)
-                    f[c] = f[p] if p != s else (FINE if chip(c) == cs and CFG["fine"] else COARSE)
                     if c in k:
                         walk(c)
         walk(s)
         kids.append(k)
-        fmt.append(f)
         when.append(w)
-    return kids, fmt, when
+    return kids, when
 
 
 def _view(T, j, name):
@@ -174,7 +148,7 @@ def _lands(topo, kids, j, c):
 
 def rank_program(g, core, T, topo):
     ranks = list(T.cores)
-    kids, fmt, when = _plan(ranks, topo)
+    kids, when = _plan(ranks, topo)
     S = T.sem
     r = T.rank_of(core)
 
@@ -190,67 +164,54 @@ def rank_program(g, core, T, topo):
         g.vector.quantize_mx(T.wq[:], T.ws[:], T.wb[:]).then_inc(S.qw, 1)
 
     sent = 0
-    flows = sorted([j for j in range(N) if core in kids[j]], key=lambda j: when[j][core])
-    for j in flows:
-        groups = _groups(topo, core, kids[j][core])
-        if j == r:
-            far = [(m, grp) for m, grp in groups if topo.chip(grp[0]) != topo.chip(core)]
-            near = [(m, grp) for m, grp in groups if topo.chip(grp[0]) == topo.chip(core)]
-            g.wait_ge(S.qx0, 1)
-            if CFG["fine"]:
-                sent += _send(g, T, topo, j, "c0", near)
-            g.wait_ge(S.qx1, 1)
-            sent += _send(g, T, topo, j, "p", groups)
-            if CFG["fine"]:
-                sent += _send(g, T, topo, j, "c1", near)
-            first = [] if CFG["fine"] else near
-            for m, grp in far:
-                for c in grp:
-                    sent += _send(g, T, topo, j, "c", [(m, [c])] + first)
-                    first = []
-            if first:
-                sent += _send(g, T, topo, j, "c", first)
+    jobs = sorted([(j != r, when[j][core] + LAG[n], n, j) for j in range(N) if core in kids[j]
+                   for n in range(len(ORDER))])
+    for foreign, t, n, j in jobs:
+        name = ORDER[n]
+        if foreign:
+            g.wait_ge(S["a%d_%s" % (j, name)], _lands(topo, kids, j, core))
         else:
-            for name in fmt[j][core]:
-                g.wait_ge(S["a%d_%s" % (j, name)], _lands(topo, kids, j, core))
-                sent += _send(g, T, topo, j, name, groups)
+            g.wait_ge(S["qx%d" % min(n, 1)], 1)
+        sent += _send(g, T, topo, j, name, _groups(topo, core, kids[j][core]))
     if sent:
         g.wait_ge(S.sent, sent)
     if r is None:
         return
 
-    order = sorted(range(N), key=lambda j: when[j][core])
+    work = [(0.0, r, 0, NC, ())]
+    for j in range(N):
+        if j != r:
+            work.append((when[j][core] + LAG[2], j, 0, MID, ("c0", "p", "c1")))
+            work.append((when[j][core] + LAG[3], j, MID, NC, ("c2",)))
+    work.sort()
     g.tensor.wait_ge(S.qw, 1)
-    for j in order:
+    for i, (t, j, lo, hi, names) in enumerate(work):
         if j == r:
             for q in range(len(CUTS)):
                 g.tensor.wait_ge(S["qx%d" % q], 1)
-        else:
-            for name in fmt[j][core]:
-                g.tensor.wait_ge(S["a%d_%s" % (j, name)], _lands(topo, kids, j, core))
-        blk = slice(j * NC, (j + 1) * NC)
-        g.tensor.matmul_mx(T.ps[:, blk], T.wq[:], T.ws[:], T.xq[:, blk], T.xs[:, blk], True, True).then_inc(S["mm%d" % j], 1)
+        for name in names:
+            g.tensor.wait_ge(S["a%d_%s" % (j, name)], _lands(topo, kids, j, core))
+        if i >= BANKS:
+            g.tensor.wait_ge(S["ev%d" % (i - BANKS)], 1)
+        b = (i % BANKS) * NC
+        cols = slice(j * NC + lo, j * NC + hi)
+        g.tensor.matmul_mx(T.ps[:, b:b + hi - lo], T.wq[:], T.ws[:], T.xq[:, cols], T.xs[:, cols],
+                           True, True).then_inc(S["mm%d" % i], 1)
     ns = na = 0
-    for n, j in enumerate(order):
-        blk = slice(j * NC, (j + 1) * NC)
-        twin = order[n ^ 1]
-        paired = CFG["pair_store"] and twin == j ^ 1
-        if n % 2 == 0:
-            g.vector.wait_ge(S["mm%d" % j], 1)
-            g.vector.tensor_copy(T.yb[:, blk], T.ps[:, blk]).then_inc(S["ev%d" % j], 1)
-            g.sync.wait_ge(S["ev%d" % j], 1)
-            if paired:
-                g.sync.wait_ge(S["ev%d" % twin], 1)
-                blk = slice(min(j, twin) * NC, (max(j, twin) + 1) * NC)
-            g.sync.dma_start(T.y[:, blk], T.yb[:, blk]).then_inc(S.st_s, 16)
+    for i, (t, j, lo, hi, names) in enumerate(work):
+        b = (i % BANKS) * NC
+        cols = slice(j * NC + lo, j * NC + hi)
+        if i % 2 == 0:
+            g.vector.wait_ge(S["mm%d" % i], 1)
+            g.vector.tensor_copy(T.yb[:, cols], T.ps[:, b:b + hi - lo]).then_inc(S["ev%d" % i], 1)
+            g.sync.wait_ge(S["ev%d" % i], 1)
+            g.sync.dma_start(T.y[:, cols], T.yb[:, cols]).then_inc(S.st_s, 16)
             ns += 16
         else:
-            g.scalar.wait_ge(S["mm%d" % j], 1)
-            g.scalar.activation(T.yb[:, blk], T.ps[:, blk], ActivationFunctionType.Copy).then_inc(S["ev%d" % j], 1)
-            if not paired:
-                g.scalar.wait_ge(S["ev%d" % j], 1)
-                g.scalar.dma_start(T.y[:, blk], T.yb[:, blk]).then_inc(S.st_a, 16)
-                na += 16
+            g.scalar.wait_ge(S["mm%d" % i], 1)
+            g.scalar.activation(T.yb[:, cols], T.ps[:, b:b + hi - lo], ActivationFunctionType.Copy).then_inc(S["ev%d" % i], 1)
+            g.scalar.wait_ge(S["ev%d" % i], 1)
+            g.scalar.dma_start(T.y[:, cols], T.yb[:, cols]).then_inc(S.st_a, 16)
+            na += 16
     g.sync.wait_ge(S.st_s, ns)
-    if na:
-        g.scalar.wait_ge(S.st_a, na)
+    g.scalar.wait_ge(S.st_a, na)

from concourse.bass import DstId, RemoteDMATransfer
from concourse.mybir import dt, ActivationFunctionType

N = 8
NC = 512
HEAD = 128
MID = 320
NCORES = 128
NCHIPS = 16
BANKS = 8
NMM = 2 * N - 1

PIECE = {"c0": ("c", 0, HEAD), "p": ("p", 0, NC), "c1": ("c", HEAD, MID), "c2": ("c", MID, NC)}
ORDER = ("c0", "p", "c1", "c2")
LAG = (0.0, 1.5, 2.0, 2.75)
CUTS = ((0, HEAD), (HEAD, NC))

SCRATCH = {
    "xb": ("sbuf", [128, 4 * NC], "bfloat16"),
    "wb": ("sbuf", [128, 512], "bfloat16"),
    "wq": ("sbuf", [128, 128], "float8_e4m3fn_x4"),
    "ws": ("sbuf", [128, 128], "uint8"),
    "xq": ("sbuf", [128, N * NC], "float8_e4m3fn_x4"),
    "xs": ("sbuf", [128, N * NC], "uint8"),
    "yb": ("sbuf", [128, N * NC], "float32"),
    "ps": ("psum", [128, BANKS * NC], "float32"),
}
SEMAPHORES = (["lw", "qw", "sent", "st_s", "st_a"]
              + ["lx%d" % i for i in range(len(CUTS))] + ["qx%d" % i for i in range(len(CUTS))]
              + ["a%d_%s" % (j, n) for j in range(N) for n in PIECE]
              + ["mm%d" % i for i in range(NMM)] + ["ev%d" % i for i in range(NMM)])


def _bits(mask):
    return bin(mask).count("1")


def _groups(topo, p, kids):
    far = [c for c in kids if topo.chip(c) != topo.chip(p)]
    near = [c for c in kids if topo.chip(c) == topo.chip(p)]
    out, far_mask = [], 0
    if far:
        far_mask = topo.mask(p, far[0])
        out.append((far_mask, far))
    if near:
        out.append((topo.mask(p, near[0]) & ~far_mask, near))
    return out


def _plan(ranks, topo):
    chip, die = topo.chip, topo.die
    homes = []
    for c in ranks:
        if chip(c) not in homes:
            homes.append(chip(c))
    at = {ch: [c for c in ranks if chip(c) == ch] for ch in homes}
    load = {}

    def free(ch, d, towards):
        ok = [c for c in range(NCORES) if chip(c) == ch and die(c) == d and c not in ranks
              and topo.may_write(c, towards)]
        c = min(ok, key=lambda c: load.get(c, 0))
        load[c] = load.get(c, 0) + 1
        return c

    gate = {}
    for s in ranks:
        other = [t for t in ranks if chip(t) != chip(s) and not topo.same_plane(chip(s), chip(t))]
        gate[s] = free(chip(s), die(s), other[0])

    kids, when = [], []
    for j, s in enumerate(ranks):
        k = {}

        def link(a, b):
            if a != b and b not in k.setdefault(a, []):
                k[a].append(b)

        def spread(a, ch):
            h = [t for t in at[ch] if die(t) == die(a)][0]
            link(a, h)
            for t in at[ch]:
                link(h, t)

        cs = chip(s)
        for t in at[cs]:
            link(s, t)
        i = homes.index(cs)
        ring = homes[i + 1:] + homes[:i]
        if die(s) != die(ranks[0]):
            ring = ring[::-1]
        for ch in ring:
            if topo.same_plane(cs, ch):
                spread(s, ch)
                continue
            m = [c for c in range(NCHIPS) if topo.mates(c, ch)][0]
            if m != cs and m not in homes:
                h = free(m, die(s), at[ch][0])
            else:
                h = gate[s]
            link(s, h)
            spread(h, ch)

        def depth(c):
            return 1 + max([depth(x) for x in k[c]]) if c in k else 0

        for p in k:
            k[p] = sorted(k[p], key=lambda c: -depth(c))
        w = {s: 0.0}

        def walk(p):
            for mask, grp in _groups(topo, p, k[p]):
                for n, c in enumerate(grp):
                    w[c] = w[p] + 1.0 + (n + 1) * (1.0 if chip(c) != chip(p) else 0.5)
                    if c in k:
                        walk(c)
        walk(s)
        kids.append(k)
        when.append(w)
    return kids, when


def _view(T, j, name):
    kind, lo, hi = PIECE[name]
    if kind == "c":
        return T.xq[:, j * NC + lo:j * NC + hi].bitcast(dt.uint8)
    return T.xs[:, j * NC + lo:j * NC + hi]


def _send(g, T, topo, j, name, groups):
    v = _view(T, j, name)
    trs = []
    for mask, grp in groups:
        ids = [DstId(rid=topo.addr(c)[0], pnc=topo.addr(c)[1]) for c in grp]
        trs.append(RemoteDMATransfer(dst_ids=ids, dma_engine_mask=mask, remote_sem=T.sem["a%d_%s" % (j, name)],
                                     srcs=[v], dsts=[v for c in grp]))
    g.remote_dma_fused(trs, local_sem=T.sem.sent)
    return sum(_bits(mask) for mask, grp in groups)


def _lands(topo, kids, j, c):
    for p in kids[j]:
        for mask, grp in _groups(topo, p, kids[j][p]):
            if c in grp:
                return _bits(mask)
    return 0


def rank_program(g, core, T, topo):
    ranks = list(T.cores)
    kids, when = _plan(ranks, topo)
    S = T.sem
    r = T.rank_of(core)

    if r is not None:
        for i, (lo, hi) in enumerate(CUTS):
            g.sync.dma_start(T.xb[:, 4 * lo:4 * hi], T.x[:, 4 * lo:4 * hi]).then_inc(S["lx%d" % i], 16)
        g.sync.dma_start(T.wb[:], T.w[:]).then_inc(S.lw, 16)
        for i, (lo, hi) in enumerate(CUTS):
            g.vector.wait_ge(S["lx%d" % i], 16)
            g.vector.quantize_mx(T.xq[:, r * NC + lo:r * NC + hi], T.xs[:, r * NC + lo:r * NC + hi],
                                 T.xb[:, 4 * lo:4 * hi]).then_inc(S["qx%d" % i], 1)
        g.vector.wait_ge(S.lw, 16)
        g.vector.quantize_mx(T.wq[:], T.ws[:], T.wb[:]).then_inc(S.qw, 1)

    sent = 0
    jobs = sorted([(j != r, when[j][core] + LAG[n], n, j) for j in range(N) if core in kids[j]
                   for n in range(len(ORDER))])
    for foreign, t, n, j in jobs:
        name = ORDER[n]
        if foreign:
            g.wait_ge(S["a%d_%s" % (j, name)], _lands(topo, kids, j, core))
        else:
            g.wait_ge(S["qx%d" % min(n, 1)], 1)
        sent += _send(g, T, topo, j, name, _groups(topo, core, kids[j][core]))
    if sent:
        g.wait_ge(S.sent, sent)
    if r is None:
        return

    work = [(0.0, r, 0, NC, ())]
    for j in range(N):
        if j != r:
            work.append((when[j][core] + LAG[2], j, 0, MID, ("c0", "p", "c1")))
            work.append((when[j][core] + LAG[3], j, MID, NC, ("c2",)))
    work.sort()
    g.tensor.wait_ge(S.qw, 1)
    for i, (t, j, lo, hi, names) in enumerate(work):
        if j == r:
            for q in range(len(CUTS)):
                g.tensor.wait_ge(S["qx%d" % q], 1)
        for name in names:
            g.tensor.wait_ge(S["a%d_%s" % (j, name)], _lands(topo, kids, j, core))
        if i >= BANKS:
            g.tensor.wait_ge(S["ev%d" % (i - BANKS)], 1)
        b = (i % BANKS) * NC
        cols = slice(j * NC + lo, j * NC + hi)
        g.tensor.matmul_mx(T.ps[:, b:b + hi - lo], T.wq[:], T.ws[:], T.xq[:, cols], T.xs[:, cols],
                           True, True).then_inc(S["mm%d" % i], 1)
    ns = na = 0
    for i, (t, j, lo, hi, names) in enumerate(work):
        b = (i % BANKS) * NC
        cols = slice(j * NC + lo, j * NC + hi)
        if i % 2 == 0:
            g.vector.wait_ge(S["mm%d" % i], 1)
            g.vector.tensor_copy(T.yb[:, cols], T.ps[:, b:b + hi - lo]).then_inc(S["ev%d" % i], 1)
            g.sync.wait_ge(S["ev%d" % i], 1)
            g.sync.dma_start(T.y[:, cols], T.yb[:, cols]).then_inc(S.st_s, 16)
            ns += 16
        else:
            g.scalar.wait_ge(S["mm%d" % i], 1)
            g.scalar.activation(T.yb[:, cols], T.ps[:, b:b + hi - lo], ActivationFunctionType.Copy).then_inc(S["ev%d" % i], 1)
            g.scalar.wait_ge(S["ev%d" % i], 1)
            g.scalar.dma_start(T.y[:, cols], T.yb[:, cols]).then_inc(S.st_a, 16)
            na += 16
    g.sync.wait_ge(S.st_s, ns)
    g.scalar.wait_ge(S.st_a, na)
